import numpy as np
import ml_dtypes


def mxq(x, axis, fmt="e4m3"):
    dtype, down = {"e4m3": (ml_dtypes.float8_e4m3fn, 7), "e5m2": (ml_dtypes.float8_e5m2, 14)}[fmt]
    v = np.moveaxis(np.asarray(x, np.float32).astype(ml_dtypes.bfloat16).astype(np.float64), axis, -1)
    blocks = v.reshape(v.shape[:-1] + (-1, 32))
    amax = np.abs(blocks).max(-1, keepdims=True)
    byte = np.maximum(np.where(amax > 0, np.frexp(amax)[1] - 1 + 127, 0) - down, 1)
    scale = np.exp2(byte - 127.0)
    codes = (blocks / scale).astype(np.float32).astype(dtype).astype(np.float64)
    return np.moveaxis((codes * scale).reshape(v.shape), -1, axis)


WIDE = False


def mx_kscale(k):
    if not WIDE:
        return np.ones(k)
    levels = np.array([10, -10, 5, -5, 0])
    if k % 512:
        return np.exp2(np.random.permutation(np.resize(levels, k // 32))).repeat(32)
    a = np.empty((k // 512, 16))
    for p in range(k // 512):
        a[p, :8] = np.random.permutation(np.resize(levels, 8))
        for g in range(8):
            far = levels[np.abs(levels - a[p, g]) >= 10]
            a[p, g + 8] = far[np.random.randint(len(far))]
    return np.exp2(a.ravel()).repeat(32)


def f64(x):
    return np.asarray(x).astype(np.float64)


def striped(idx):
    return np.tile(idx.reshape(-1, 16).T, (8, 1)).astype(np.uint16)


def unstriped(offs):
    return offs[:16].T.reshape(-1).astype(np.int64)


def striped8(idx):
    return np.concatenate([x.reshape(-1, 16).T for x in idx]).astype(np.uint16)


def runs(offs, k):
    lists = np.stack([offs[16 * r : 16 * r + 16].T.reshape(-1) for r in range(8)]).astype(np.int64)
    return lists[np.arange(k) % 512 // 64]


def pack_weight(w):
    k, n = w.shape
    w = f64(np.asarray(w, np.float32).astype(ml_dtypes.bfloat16)).reshape(k // 32, 32, n)
    amax = np.abs(w).max(1)
    byte = np.clip(np.where(amax > 0, np.frexp(amax)[1] - 1 + 127 - 7, 1), 1, 254)
    scaled = (w * np.exp2(127.0 - byte)[:, None, :]).reshape(k, n).astype(np.float32)
    words = np.ascontiguousarray(scaled.reshape(k // 512, 128, 4, n).transpose(0, 1, 3, 2)).astype(ml_dtypes.float8_e4m3fn).view(np.uint8)
    return words, np.ascontiguousarray(byte.astype(np.uint8).reshape(k // 512, 16, n))


def unpack_weight(words, scales):
    g, p, n, _ = words.shape
    vals = np.ascontiguousarray(words).view(ml_dtypes.float8_e4m3fn).astype(np.float64) * np.repeat(np.exp2(scales.astype(np.float64) - 127.0), 8, axis=1)[..., None]
    return vals.transpose(0, 1, 3, 2).reshape(g * 512, n)


def relu(v):
    return np.maximum(v, 0.0)

def planes(y):
    n, m = y.shape
    v = y.astype(np.float32).astype(ml_dtypes.bfloat16).astype(np.float64).reshape(n // 32, 32, m)
    top = np.abs(v).max(1)
    byte = np.clip(np.where(top > 0, np.frexp(top)[1] - 1 + 127 - 7, 1), 1, 254)
    codes = (v * np.exp2(127.0 - byte)[:, None, :]).reshape(n, m).astype(np.float32).astype(ml_dtypes.float8_e4m3fn).view(np.uint8)
    words = codes.reshape(n // 512, 128, 4, m).transpose(0, 1, 3, 2)
    return np.ascontiguousarray(words), np.ascontiguousarray(byte.astype(np.uint8).reshape(n // 512, 16, m))


K, T, S, N, H = 512, 2048, 512, 512, 512


def setup_inputs():
    n = np.random.standard_normal
    s = mx_kscale(K)[:, None]
    u = mx_kscale(H)
    packed_xT = pack_weight(n((K, T)) * s)
    packed_w1 = pack_weight(n((K, H)) / np.sqrt(K) / s)
    packed_w2 = pack_weight(n((H, N)) / np.sqrt(2 * H) / u[:, None])
    packed_w3 = pack_weight(n((H, N)) / np.sqrt(2 * H) / u[:, None])
    return {
        "x_words": packed_xT[0],
        "x_scales": packed_xT[1],
        "w1_words": packed_w1[0],
        "w1_scales": packed_w1[1],
        "gn": (np.random.uniform(0.5, 1.5, (H, 1)) * u[:, None]).astype(np.float32),
        "gm": (np.random.uniform(0.5, 1.5, (H, 1)) * u[:, None]).astype(np.float32),
        "w2_words": packed_w2[0],
        "w2_scales": packed_w2[1],
        "w3_words": packed_w3[0],
        "w3_scales": packed_w3[1],
        "offs": striped(np.random.permutation(T)[:S]),
        "n1": striped8(np.stack([np.random.permutation(S) for _ in range(8)])),
        "n2": striped8(np.stack([np.random.permutation(S) for _ in range(8)])),
        "n3": striped8(np.stack([np.random.permutation(S) for _ in range(8)])),
        "n4": striped8(np.stack([np.random.permutation(S) for _ in range(8)])),
        "n5": striped8(np.stack([np.random.permutation(S) for _ in range(8)])),
        "n6": striped8(np.stack([np.random.permutation(S) for _ in range(8)])),
    }


def reference(x_words, x_scales, w1_words, w1_scales, gn, gm, w2_words, w2_scales, w3_words, w3_scales, offs, n1, n2, n3, n4, n5, n6):
    xq = unpack_weight(x_words, x_scales)[:, unstriped(offs)]
    y = unpack_weight(w1_words, w1_scales).T @ xq
    z = f64(gn) * (np.minimum(np.maximum(y, y[np.arange(H)[:, None], runs(n1, H)]), y[np.arange(H)[:, None], runs(n2, H)]))
    z2 = f64(gm) * (relu(y - (y[np.arange(H)[:, None], runs(n3, H)])) + 0.5 * (relu(y[np.arange(H)[:, None], runs(n4, H)] - y)))
    h = unpack_weight(w2_words, w2_scales).T @ mxq(z, 0, "e4m3") + unpack_weight(w3_words, w3_scales).T @ mxq(z2, 0, "e4m3")
    out_0 = 0.75 * (h[np.arange(N)[:, None], runs(n5, N)] + h[np.arange(N)[:, None], runs(n6, N)]) - h
    return (out_0,) + planes(out_0)

@@ -1,0 +1,229 @@
+from contextlib import ExitStack
+
+import concourse.mybir as mybir
+
+F32 = mybir.dt.float32
+BF16 = mybir.dt.bfloat16
+I32 = mybir.dt.int32
+U32 = mybir.dt.uint32
+U16 = mybir.dt.uint16
+U8 = mybir.dt.uint8
+FP8X4 = mybir.dt.float8_e4m3fn_x4
+ALU = mybir.AluOpType
+ACT = mybir.ActivationFunctionType
+
+P = 128
+PACK = 4
+T = 2048
+S = 512
+FLOPS = 3 * 2 * 512 * 512 * 512
+CH1 = ((0, 256), (256, 128), (384, 128))
+CH2 = ((0, 256), (256, 128), (384, 128))
+
+
+def words_of(ap):
+    return ap[0].rearrange("p n t -> p (n t)").bitcast(I32)
+
+
+def weave(flat):
+    return flat.rearrange("p (c i t) -> p c t i", i=4, t=PACK)
+
+
+def planar(tile3):
+    return tile3.rearrange("p t (c i) -> p c t i", i=4)
+
+
+def tile_picked_joinminmxhingelap_none_po_kernel(
+    tc, x_words, x_scales, w1_words, w1_scales, gn, gm, w2_words, w2_scales, w3_words, w3_scales,
+    offs, n1, n2, n3, n4, n5, n6, out_0, out_1, out_2,
+):
+    nc = tc.nc
+    with ExitStack() as ctx:
+        keep = ctx.enter_context(tc.tile_pool(name="keep", bufs=1))
+        psum = ctx.enter_context(tc.psum_pool(name="psum", bufs=1))
+
+        def load_list(name, src):
+            tile = keep.tile([P, S // 16], U16, name=name)
+            nc.sync.dma_start(tile[:], src)
+            return tile
+
+        def load_scales(queue, tile, src, k):
+            for q in range(4):
+                queue.dma_start(tile[32 * q + k : 32 * q + k + 4, :].bitcast(I32), src[0][4 * q : 4 * q + 4, :].bitcast(I32))
+
+        xs = keep.tile([P, T], U8, name="xs", align_bytes=64)
+        w1s_raw = keep.tile([P, S], U8, name="w1s_raw", align_bytes=64)
+        w23s_raw = keep.tile([P, S], U8, name="w23s_raw", align_bytes=64)
+        nc.gpsimd.memset(w1s_raw[:].bitcast(I32), 0)
+        nc.vector.memset(xs[:].bitcast(I32), 0)
+
+        xw = keep.tile([P, T], U32, name="xw", align_bytes=64)
+        w1w_raw = keep.tile([P, S], I32, name="w1w_raw", align_bytes=64)
+        w23w_raw = keep.tile([P, 2, S], I32, name="w23w_raw", align_bytes=64)
+        gn_sb = keep.tile([P, PACK], F32, name="gn_sb")
+        gm_sb = keep.tile([P, PACK], F32, name="gm_sb")
+
+        nc.scalar.dma_start(xw[:].bitcast(I32), words_of(x_words))
+        offs_sb = load_list("offs_sb", offs)
+        nc.sync.dma_start(w1w_raw[:], words_of(w1_words))
+        load_scales(nc.gpsimd, w1s_raw, w1_scales, 0)
+        nc.gpsimd.memset(w23s_raw[:].bitcast(I32), 0)
+        load_scales(nc.sync, xs, x_scales, 0)
+        l1 = load_list("l1", n1)
+        l2 = load_list("l2", n2)
+        l4 = load_list("l4", n4)
+        l3 = load_list("l3", n3)
+        nc.sync.dma_start(gm_sb[:], gm.rearrange("(p t) o -> p (t o)", t=PACK))
+        nc.sync.dma_start(gn_sb[:], gn.rearrange("(p t) o -> p (t o)", t=PACK))
+        nc.sync.dma_start(w23w_raw[:, 0, :], words_of(w2_words))
+        nc.sync.dma_start(w23w_raw[:, 1, :], words_of(w3_words))
+        load_scales(nc.sync, w23s_raw, w2_scales, 0)
+        load_scales(nc.sync, w23s_raw, w3_scales, 4)
+        l5 = load_list("l5", n5)
+        l6 = load_list("l6", n6)
+
+        neg_gm = keep.tile([P, PACK], F32, name="neg_gm")
+        nc.scalar.activation(neg_gm[:], gm_sb[:], ACT.Copy, scale=-1.0)
+
+        w1w = keep.tile([P, S], I32, name="w1w", align_bytes=64)
+        w1s = keep.tile([P, S], U8, name="w1s", align_bytes=64)
+        nc.vector.tensor_copy(w1w[:].rearrange("p (t m) -> p m t", t=PACK), w1w_raw[:].rearrange("p (m t) -> p m t", t=PACK))
+        nc.vector.tensor_copy(w1s[:].rearrange("p (t m) -> p t m", t=PACK), w1s_raw[:].rearrange("p (m t) -> p t m", t=PACK))
+
+        xgs = keep.tile([P, S], U8, name="xgs", align_bytes=64)
+        xgw = keep.tile([P, S], U32, name="xgw", align_bytes=64)
+        nc.vector.tensor_copy(xgs[:], xs[:].indirect(offs_sb[:]))
+        y_ps = [psum.tile([P, S], F32, name="y_ps%d" % t) for t in range(PACK)]
+        h_ps = [psum.tile([P, S], F32, name="h_ps%d" % t) for t in range(PACK)]
+        y_win = [keep.tile([P, S], F32, name="y_win%d" % t) for t in range(PACK)]
+        y4 = keep.tile([P, PACK, S], F32, name="y4")
+        for half in range(2):
+            cols = slice(256 * half, 256 * half + 256)
+            nc.vector.tensor_copy(xgw[:, cols], xw[:].indirect(offs_sb[:, 16 * half : 16 * half + 16]))
+            for t in range(PACK):
+                ms = slice(P * t, P * t + P)
+                nc.tensor.matmul_mx(
+                    y_ps[t][:, cols], lhsT=w1w[:, ms].bitcast(FP8X4), lhsT_scale=w1s[:, ms],
+                    rhs=xgw[:, cols].bitcast(FP8X4), rhs_scale=xgs[:, cols], start=True, stop=True,
+                )
+        for half in range(2):
+            cols = slice(256 * half, 256 * half + 256)
+            nc.scalar.copy(y_win[0][:, cols], y_ps[0][:, cols])
+        for t in range(1, PACK):
+            nc.scalar.copy(y_win[t][:], y_ps[t][:])
+        for t in range(PACK):
+            nc.scalar.copy(y4[:, t, :], y_ps[t][:])
+
+        w23w = keep.tile([P, 2, S], I32, name="w23w", align_bytes=64)
+        w23s = keep.tile([P, S], U8, name="w23s", align_bytes=64)
+        nc.gpsimd.tensor_copy(
+            w23w[:].rearrange("p g (t m) -> p g m t", t=PACK), w23w_raw[:].rearrange("p g (m t) -> p g m t", t=PACK)
+        )
+        nc.gpsimd.tensor_copy(w23s[:].rearrange("p (t m) -> p t m", t=PACK), w23s_raw[:].rearrange("p (m t) -> p t m", t=PACK))
+
+        h_win = [keep.tile([P, S], F32, name="h_win%d" % t) for t in range(PACK)]
+        h4 = keep.tile([P, PACK, S], F32, name="h4")
+        zw = keep.tile([P, S], U32, name="zw", align_bytes=64)
+        zs = keep.tile([P, S], U8, name="zs", align_bytes=64)
+        z2w = keep.tile([P, S], U32, name="z2w", align_bytes=64)
+        z2s = keep.tile([P, S], U8, name="z2s", align_bytes=64)
+
+        def f32_chunk(name, n):
+            return keep.tile([P, PACK, n], F32, name=name)
+
+        def gain_and_weave(name, src, gain, n, last):
+            woven = keep.tile([P, PACK * n], BF16, name=name + "_woven", align_bytes=64)
+            if last:
+                spread = gain[:].rearrange("p (c t i) -> p c t i", c=1, i=1).to_broadcast([P, n // 4, PACK, 4])
+                nc.vector.tensor_tensor(weave(woven[:]), planar(src[:]), spread, ALU.mult)
+                return woven
+            flat = keep.tile([P, PACK, n], BF16, name=name + "_flat")
+            for t in range(PACK):
+                nc.scalar.activation(flat[:, t, :], src[:, t, :], ACT.Copy, scale=gain[:, t : t + 1])
+            nc.scalar.copy(weave(woven[:]), planar(flat[:]))
+            return woven
+
+        def second_product(c0, n, z_woven, z2_woven):
+            cols = slice(c0, c0 + n)
+            nc.vector.quantize_mx(zw[:, cols].bitcast(FP8X4), zs[:, cols], z_woven[:])
+            nc.vector.quantize_mx(z2w[:, cols].bitcast(FP8X4), z2s[:, cols], z2_woven[:])
+            for t in range(PACK):
+                ms = slice(P * t, P * t + P)
+                nc.tensor.matmul_mx(
+                    h_ps[t][:, cols], lhsT=w23w[:, 0, ms].bitcast(FP8X4), lhsT_scale=w23s[:, ms],
+                    rhs=zw[:, cols].bitcast(FP8X4), rhs_scale=zs[:, cols], start=True, stop=False,
+                )
+                nc.tensor.matmul_mx(
+                    h_ps[t][:, cols], lhsT=w23w[:, 1, ms].bitcast(FP8X4), lhsT_scale=w23s[4:P, ms],
+                    rhs=z2w[:, cols].bitcast(FP8X4), rhs_scale=z2s[:, cols], start=False, stop=True,
+                )
+            for t in range(PACK):
+                nc.scalar.activation(h_win[t][:, cols], h_ps[t][:, cols], ACT.Copy, scale=0.75)
+            for t in range(PACK):
+                nc.scalar.copy(h4[:, t, cols], h_ps[t][:, cols])
+
+        pending = None
+        for c0, n in CH1:
+            cols = slice(c0, c0 + n)
+            ks = slice(c0 // 16, (c0 + n) // 16)
+            tag = "_%d" % c0
+            u = f32_chunk("u" + tag, n)
+            v = f32_chunk("v" + tag, n)
+            a = f32_chunk("a" + tag, n)
+            b = f32_chunk("b" + tag, n)
+            r = f32_chunk("r" + tag, n)
+            last = c0 + n == S
+            for t in range(PACK):
+                nc.vector.tensor_copy(a[:, t, :], y_win[t][:].indirect(l1[:, ks]))
+            for t in range(PACK):
+                nc.vector.tensor_copy(b[:, t, :], y_win[t][:].indirect(l2[:, ks]))
+            nc.vector.tensor_tensor(a[:], a[:], y4[:, :, cols], ALU.max)
+            if pending is not None:
+                second_product(*pending)
+            for t in range(2):
+                nc.vector.tensor_tensor(v[:, t, :], y_win[t][:].indirect(l4[:, ks]), y4[:, t, cols], ALU.subtract)
+            nc.vector.tensor_tensor(a[:], a[:], b[:], ALU.min)
+            for t in range(2, PACK):
+                nc.vector.tensor_tensor(v[:, t, :], y_win[t][:].indirect(l4[:, ks]), y4[:, t, cols], ALU.subtract)
+            nc.scalar.activation(r[:], v[:], ACT.Relu, scale=0.5)
+            z_woven = gain_and_weave("z" + tag, a, gn_sb, n, False)
+            for t in range(PACK):
+                nc.vector.tensor_tensor(u[:, t, :], y_win[t][:].indirect(l3[:, ks]), y4[:, t, cols], ALU.subtract)
+            nc.vector.scalar_tensor_tensor(u[:], u[:], 0.0, r[:], ALU.min, ALU.subtract)
+            z2_woven = gain_and_weave("z2" + tag, u, neg_gm, n, last)
+            pending = (c0, n, z_woven, z2_woven)
+        second_product(*pending)
+
+        ow = keep.tile([P, S], U32, name="ow", align_bytes=64)
+        osc = keep.tile([P, S], U8, name="osc", align_bytes=64)
+        out_rows = out_0.rearrange("(p t) j -> p t j", t=PACK)
+
+        def planes(c0, n, woven):
+            cols = slice(c0, c0 + n)
+            nc.vector.quantize_mx(ow[:, cols].bitcast(FP8X4), osc[:, cols], woven[:])
+            nc.sync.dma_start(words_of(out_1)[:, cols], ow[:, cols].bitcast(I32))
+
+        pending = None
+        for c0, n in CH2:
+            cols = slice(c0, c0 + n)
+            ks = slice(c0 // 16, (c0 + n) // 16)
+            tag = "_%d" % c0
+            g = f32_chunk("g" + tag, n)
+            o = f32_chunk("o" + tag, n)
+            woven = keep.tile([P, PACK * n], BF16, name="o_woven" + tag, align_bytes=64)
+            for t in range(PACK):
+                nc.vector.tensor_tensor(g[:, t, :], h_win[t][:].indirect(l5[:, ks]), h4[:, t, cols], ALU.subtract)
+            for t in range(PACK):
+                nc.vector.tensor_tensor(o[:, t, :], h_win[t][:].indirect(l6[:, ks]), g[:, t, :], ALU.add)
+            if pending is not None:
+                planes(*pending)
+            nc.sync.dma_start(out_rows[:, :, cols], o[:])
+            if c0 + n == S:
+                nc.vector.tensor_copy(weave(woven[:]), planar(o[:]))
+            else:
+                nc.scalar.copy(weave(woven[:]), planar(o[:]))
+            pending = (c0, n, woven)
+        planes(*pending)
+        for q in range(4):
+            queue = nc.scalar if q % 2 else nc.sync
+            queue.dma_start(out_2[0][4 * q : 4 * q + 4, :].bitcast(I32), osc[32 * q : 32 * q + 4, :].bitcast(I32))

@@ -1,6 +1,7 @@
 from contextlib import ExitStack
 
 import concourse.mybir as mybir
+from concourse.masks import make_identity
 
 F32 = mybir.dt.float32
 BF16 = mybir.dt.bfloat16
@@ -17,8 +18,9 @@ PACK = 4
 T = 2048
 S = 512
 FLOPS = 3 * 2 * 512 * 512 * 512
-CH1 = ((0, 256), (256, 128), (384, 128))
-CH2 = ((0, 256), (256, 128), (384, 128))
+HALF = 256
+HEAD = 384
+PIECES = ((0, 256), (256, 128), (384, 128))
 
 
 def words_of(ap):
@@ -40,39 +42,49 @@ def tile_picked_joinminmxhingelap_none_po_kernel(
     nc = tc.nc
     with ExitStack() as ctx:
         keep = ctx.enter_context(tc.tile_pool(name="keep", bufs=1))
-        psum = ctx.enter_context(tc.psum_pool(name="psum", bufs=1))
+        ring = ctx.enter_context(tc.psum_pool(name="ring", bufs=8))
+        work = ctx.enter_context(tc.tile_pool(name="work", bufs=1))
 
         def load_list(name, src):
             tile = keep.tile([P, S // 16], U16, name=name)
             nc.sync.dma_start(tile[:], src)
             return tile
 
-        def load_scales(queue, tile, src, k):
-            for q in range(4):
+        def load_scales(queue, tile, src, k, quadrants=(0, 1, 2, 3)):
+            for q in quadrants:
                 queue.dma_start(tile[32 * q + k : 32 * q + k + 4, :].bitcast(I32), src[0][4 * q : 4 * q + 4, :].bitcast(I32))
 
         xs = keep.tile([P, T], U8, name="xs", align_bytes=64)
         w1s_raw = keep.tile([P, S], U8, name="w1s_raw", align_bytes=64)
         w23s_raw = keep.tile([P, S], U8, name="w23s_raw", align_bytes=64)
-        nc.gpsimd.memset(w1s_raw[:].bitcast(I32), 0)
-        nc.vector.memset(xs[:].bitcast(I32), 0)
+        nc.gpsimd.memset(xs[:].bitcast(I32), 0)
+        nc.vector.memset(w1s_raw[:].bitcast(I32), 0)
 
+        y_win = [keep.tile([P, 2 * S], F32, name="y_win%d" % t) for t in range(PACK)]
+        h_win = [keep.tile([P, 2 * S], F32, name="h_win%d" % t) for t in range(PACK)]
+        for t in range(PACK):
+            nc.vector.memset(y_win[t][:, S:], 0.0)
         xw = keep.tile([P, T], U32, name="xw", align_bytes=64)
         w1w_raw = keep.tile([P, S], I32, name="w1w_raw", align_bytes=64)
         w23w_raw = keep.tile([P, 2, S], I32, name="w23w_raw", align_bytes=64)
         gn_sb = keep.tile([P, PACK], F32, name="gn_sb")
         gm_sb = keep.tile([P, PACK], F32, name="gm_sb")
 
-        nc.scalar.dma_start(xw[:].bitcast(I32), words_of(x_words))
         offs_sb = load_list("offs_sb", offs)
         nc.sync.dma_start(w1w_raw[:], words_of(w1_words))
-        load_scales(nc.gpsimd, w1s_raw, w1_scales, 0)
-        nc.gpsimd.memset(w23s_raw[:].bitcast(I32), 0)
+        l3 = load_list("l3", n3)
+        l4 = load_list("l4", n4)
+        nc.sync.dma_start(xw[:].bitcast(I32), words_of(x_words))
         load_scales(nc.sync, xs, x_scales, 0)
+        load_scales(nc.gpsimd, w1s_raw, w1_scales, 0, (0, 1))
+        load_scales(nc.sync, w1s_raw, w1_scales, 0, (2, 3))
+        nc.gpsimd.memset(w23s_raw[:].bitcast(I32), 0)
+        ident = keep.tile([P, P], F32, name="ident")
+        make_identity(nc, ident[:])
+        for t in range(PACK):
+            nc.gpsimd.memset(h_win[t][:, S:], 0.0)
         l1 = load_list("l1", n1)
         l2 = load_list("l2", n2)
-        l4 = load_list("l4", n4)
-        l3 = load_list("l3", n3)
         nc.sync.dma_start(gm_sb[:], gm.rearrange("(p t) o -> p (t o)", t=PACK))
         nc.sync.dma_start(gn_sb[:], gn.rearrange("(p t) o -> p (t o)", t=PACK))
         nc.sync.dma_start(w23w_raw[:, 0, :], words_of(w2_words))
@@ -82,9 +94,6 @@ def tile_picked_joinminmxhingelap_none_po_kernel(
         l5 = load_list("l5", n5)
         l6 = load_list("l6", n6)
 
-        neg_gm = keep.tile([P, PACK], F32, name="neg_gm")
-        nc.scalar.activation(neg_gm[:], gm_sb[:], ACT.Copy, scale=-1.0)
-
         w1w = keep.tile([P, S], I32, name="w1w", align_bytes=64)
         w1s = keep.tile([P, S], U8, name="w1s", align_bytes=64)
         nc.vector.tensor_copy(w1w[:].rearrange("p (t m) -> p m t", t=PACK), w1w_raw[:].rearrange("p (m t) -> p m t", t=PACK))
@@ -93,26 +102,33 @@ def tile_picked_joinminmxhingelap_none_po_kernel(
         xgs = keep.tile([P, S], U8, name="xgs", align_bytes=64)
         xgw = keep.tile([P, S], U32, name="xgw", align_bytes=64)
         nc.vector.tensor_copy(xgs[:], xs[:].indirect(offs_sb[:]))
-        y_ps = [psum.tile([P, S], F32, name="y_ps%d" % t) for t in range(PACK)]
-        h_ps = [psum.tile([P, S], F32, name="h_ps%d" % t) for t in range(PACK)]
-        y_win = [keep.tile([P, S], F32, name="y_win%d" % t) for t in range(PACK)]
-        y4 = keep.tile([P, PACK, S], F32, name="y4")
+        y_ps = [ring.tile([P, S], F32, name="y_ps%d" % t, tag="ring") for t in range(PACK)]
+        neg_y = keep.tile([P, PACK, S], F32, name="neg_y")
+        def first_product(t, cols):
+            ms = slice(P * t, P * t + P)
+            nc.tensor.matmul_mx(
+                y_ps[t][:, cols], lhsT=w1w[:, ms].bitcast(FP8X4), lhsT_scale=w1s[:, ms],
+                rhs=xgw[:, cols].bitcast(FP8X4), rhs_scale=xgs[:, cols], start=True, stop=True,
+            )
+
         for half in range(2):
             cols = slice(256 * half, 256 * half + 256)
             nc.vector.tensor_copy(xgw[:, cols], xw[:].indirect(offs_sb[:, 16 * half : 16 * half + 16]))
-            for t in range(PACK):
-                ms = slice(P * t, P * t + P)
-                nc.tensor.matmul_mx(
-                    y_ps[t][:, cols], lhsT=w1w[:, ms].bitcast(FP8X4), lhsT_scale=w1s[:, ms],
-                    rhs=xgw[:, cols].bitcast(FP8X4), rhs_scale=xgs[:, cols], start=True, stop=True,
-                )
+            for t in range(2):
+                first_product(t, cols)
+        for t in range(2, PACK):
+            first_product(t, slice(0, S))
         for half in range(2):
             cols = slice(256 * half, 256 * half + 256)
             nc.scalar.copy(y_win[0][:, cols], y_ps[0][:, cols])
-        for t in range(1, PACK):
-            nc.scalar.copy(y_win[t][:], y_ps[t][:])
         for t in range(PACK):
-            nc.scalar.copy(y4[:, t, :], y_ps[t][:])
+            if t > 0:
+                nc.scalar.copy(y_win[t][:, :S], y_ps[t][:])
+            nc.scalar.activation(neg_y[:, t, :], y_ps[t][:], ACT.Copy, scale=-1.0)
+
+        y_small = [keep.tile([P, S], F32, name="y_small%d" % t) for t in range(PACK)]
+        for t in range(PACK):
+            nc.sync.dma_start(y_small[t][:], y_win[t][:, :S])
 
         w23w = keep.tile([P, 2, S], I32, name="w23w", align_bytes=64)
         w23s = keep.tile([P, S], U8, name="w23s", align_bytes=64)
@@ -121,78 +137,99 @@ def tile_picked_joinminmxhingelap_none_po_kernel(
         )
         nc.gpsimd.tensor_copy(w23s[:].rearrange("p (t m) -> p t m", t=PACK), w23s_raw[:].rearrange("p (m t) -> p t m", t=PACK))
 
-        h_win = [keep.tile([P, S], F32, name="h_win%d" % t) for t in range(PACK)]
         h4 = keep.tile([P, PACK, S], F32, name="h4")
         zw = keep.tile([P, S], U32, name="zw", align_bytes=64)
         zs = keep.tile([P, S], U8, name="zs", align_bytes=64)
         z2w = keep.tile([P, S], U32, name="z2w", align_bytes=64)
         z2s = keep.tile([P, S], U8, name="z2s", align_bytes=64)
 
-        def f32_chunk(name, n):
-            return keep.tile([P, PACK, n], F32, name=name)
+        def f32_chunk(name, n, tag=None):
+            return work.tile([P, PACK, n], F32, name=name, tag=tag or name, align_bytes=64)
 
-        def gain_and_weave(name, src, gain, n, last):
-            woven = keep.tile([P, PACK * n], BF16, name=name + "_woven", align_bytes=64)
-            if last:
-                spread = gain[:].rearrange("p (c t i) -> p c t i", c=1, i=1).to_broadcast([P, n // 4, PACK, 4])
-                nc.vector.tensor_tensor(weave(woven[:]), planar(src[:]), spread, ALU.mult)
-                return woven
-            flat = keep.tile([P, PACK, n], BF16, name=name + "_flat")
-            for t in range(PACK):
-                nc.scalar.activation(flat[:, t, :], src[:, t, :], ACT.Copy, scale=gain[:, t : t + 1])
-            nc.scalar.copy(weave(woven[:]), planar(flat[:]))
-            return woven
+        def woven_tile(name, n):
+            return work.tile([P, PACK * n], BF16, name=name, tag=name, align_bytes=64)
 
-        def second_product(c0, n, z_woven, z2_woven):
+        c = f32_chunk("c", S)
+        d = f32_chunk("d", S)
+        z2_flat = work.tile([P, PACK, S], BF16, name="z2_flat", tag="z2_flat")
+        for t in range(PACK):
+            hinges = []
+            for got, lst, scale, name in ((c, l3, -1.0, "c"), (d, l4, 0.5, "d")):
+                diff = ring.tile([P, PACK, P], F32, name="diff", tag="ring")
+                nc.vector.tensor_copy(got[:, t, :], y_win[t][:].indirect(lst[:]))
+                for j in range(PACK):
+                    js = slice(P * j, P * j + P)
+                    nc.tensor.matmul(diff[:, j, :], neg_y[:, t, js], ident[:], start=True, stop=False, is_transpose=True)
+                    nc.tensor.matmul(diff[:, j, :], got[:, t, js], ident[:], start=False, stop=True, is_transpose=True)
+                hinge = work.tile([P, PACK, P], F32, name="hinge_%s%d" % (name, t))
+                nc.scalar.activation(hinge[:], diff[:], ACT.Relu, scale=scale)
+                hinges.append(hinge)
+            back = ring.tile([P, S], F32, name="back", tag="ring")
+            for j in range(PACK):
+                for k in range(2):
+                    nc.tensor.matmul(back[:, P * j : P * j + P], hinges[k][:, j, :], ident[:],
+                                     start=k == 0, stop=k == 1, is_transpose=True)
+            nc.scalar.activation(z2_flat[:, t, :], back[:], ACT.Copy, scale=gm_sb[:, t : t + 1])
+        z2_woven = woven_tile("z2_woven", S)
+        nc.scalar.copy(weave(z2_woven[:]), planar(z2_flat[:]))
+
+        h_ps = [ring.tile([P, S], F32, name="h_ps%d" % t, tag="ring") for t in range(PACK)]
+
+        def second_product(c0, n, z_woven):
             cols = slice(c0, c0 + n)
             nc.vector.quantize_mx(zw[:, cols].bitcast(FP8X4), zs[:, cols], z_woven[:])
-            nc.vector.quantize_mx(z2w[:, cols].bitcast(FP8X4), z2s[:, cols], z2_woven[:])
+            for t in range(PACK):
+                ms = slice(P * t, P * t + P)
+                nc.tensor.matmul_mx(
+                    h_ps[t][:, cols], lhsT=w23w[:, 1, ms].bitcast(FP8X4), lhsT_scale=w23s[4:P, ms],
+                    rhs=z2w[:, cols].bitcast(FP8X4), rhs_scale=z2s[:, cols], start=True, stop=False,
+                )
             for t in range(PACK):
                 ms = slice(P * t, P * t + P)
                 nc.tensor.matmul_mx(
                     h_ps[t][:, cols], lhsT=w23w[:, 0, ms].bitcast(FP8X4), lhsT_scale=w23s[:, ms],
-                    rhs=zw[:, cols].bitcast(FP8X4), rhs_scale=zs[:, cols], start=True, stop=False,
+                    rhs=zw[:, cols].bitcast(FP8X4), rhs_scale=zs[:, cols], start=False, stop=True,
                 )
-                nc.tensor.matmul_mx(
-                    h_ps[t][:, cols], lhsT=w23w[:, 1, ms].bitcast(FP8X4), lhsT_scale=w23s[4:P, ms],
-                    rhs=z2w[:, cols].bitcast(FP8X4), rhs_scale=z2s[:, cols], start=False, stop=True,
-                )
-            for t in range(PACK):
-                nc.scalar.activation(h_win[t][:, cols], h_ps[t][:, cols], ACT.Copy, scale=0.75)
-            for t in range(PACK):
-                nc.scalar.copy(h4[:, t, cols], h_ps[t][:, cols])
 
-        pending = None
-        for c0, n in CH1:
-            cols = slice(c0, c0 + n)
-            ks = slice(c0 // 16, (c0 + n) // 16)
-            tag = "_%d" % c0
-            u = f32_chunk("u" + tag, n)
-            v = f32_chunk("v" + tag, n)
-            a = f32_chunk("a" + tag, n)
-            b = f32_chunk("b" + tag, n)
-            r = f32_chunk("r" + tag, n)
-            last = c0 + n == S
-            for t in range(PACK):
-                nc.vector.tensor_copy(a[:, t, :], y_win[t][:].indirect(l1[:, ks]))
-            for t in range(PACK):
-                nc.vector.tensor_copy(b[:, t, :], y_win[t][:].indirect(l2[:, ks]))
-            nc.vector.tensor_tensor(a[:], a[:], y4[:, :, cols], ALU.max)
-            if pending is not None:
-                second_product(*pending)
-            for t in range(2):
-                nc.vector.tensor_tensor(v[:, t, :], y_win[t][:].indirect(l4[:, ks]), y4[:, t, cols], ALU.subtract)
-            nc.vector.tensor_tensor(a[:], a[:], b[:], ALU.min)
-            for t in range(2, PACK):
-                nc.vector.tensor_tensor(v[:, t, :], y_win[t][:].indirect(l4[:, ks]), y4[:, t, cols], ALU.subtract)
-            nc.scalar.activation(r[:], v[:], ACT.Relu, scale=0.5)
-            z_woven = gain_and_weave("z" + tag, a, gn_sb, n, False)
-            for t in range(PACK):
-                nc.vector.tensor_tensor(u[:, t, :], y_win[t][:].indirect(l3[:, ks]), y4[:, t, cols], ALU.subtract)
-            nc.vector.scalar_tensor_tensor(u[:], u[:], 0.0, r[:], ALU.min, ALU.subtract)
-            z2_woven = gain_and_weave("z2" + tag, u, neg_gm, n, last)
-            pending = (c0, n, z_woven, z2_woven)
-        second_product(*pending)
+        def leave_bank(t, cols):
+            nc.scalar.activation(h_win[t][:, cols], h_ps[t][:, cols], ACT.Copy, scale=0.75)
+            nc.scalar.copy(h4[:, t, cols], h_ps[t][:, cols])
+
+        a = f32_chunk("a", S)
+        for t in range(PACK):
+            nc.vector.tensor_copy(a[:, t, :], y_win[t][:].indirect(l1[:]))
+        b0 = f32_chunk("b0", HEAD)
+        z_flat = work.tile([P, PACK, HEAD], BF16, name="z_flat", tag="z2_flat")
+        for t in range(PACK):
+            nc.vector.tensor_copy(b0[:, t, :], y_win[t][:].indirect(l2[:, : HEAD // 16]))
+            nc.vector.tensor_tensor(a[:, t, :], a[:, t, :], y_win[t][:, :S], ALU.max)
+            if t > 0:
+                nc.vector.tensor_tensor(b0[:, t - 1, :], b0[:, t - 1, :], a[:, t - 1, :HEAD], ALU.min)
+        nc.vector.quantize_mx(z2w[:].bitcast(FP8X4), z2s[:], z2_woven[:])
+        nc.vector.tensor_tensor(b0[:, 3, :], b0[:, 3, :], a[:, 3, :HEAD], ALU.min)
+        for t in range(PACK):
+            nc.scalar.activation(z_flat[:, t, :], b0[:, t, :], ACT.Copy, scale=gn_sb[:, t : t + 1])
+        z_woven = [woven_tile("z_woven%d" % c0, n) for c0, n in PIECES]
+        for k in range(2):
+            c0, n = PIECES[k]
+            nc.scalar.copy(weave(z_woven[k][:]), planar(z_flat[:, :, c0 : c0 + n]))
+        b1 = f32_chunk("b1", S - HEAD, "z2_woven")
+        for t in range(PACK):
+            nc.vector.tensor_copy(b1[:, t, :], y_small[t][:].indirect(l2[:, HEAD // 16 :]))
+        second_product(*PIECES[0], z_woven[0])
+        low = f32_chunk("low", S - HEAD, "z_woven0")
+        nc.vector.tensor_tensor(low[:], b1[:], a[:, :, HEAD:], ALU.min)
+        second_product(*PIECES[1], z_woven[1])
+        leave_bank(0, slice(0, HEAD))
+        spread = gn_sb[:].rearrange("p (c t i) -> p c t i", c=1, i=1).to_broadcast([P, (S - HEAD) // 4, PACK, 4])
+        nc.vector.tensor_tensor(weave(z_woven[2][:]), planar(low[:]), spread, ALU.mult)
+        second_product(*PIECES[2], z_woven[2])
+        leave_bank(0, slice(HEAD, S))
+        for t in range(1, PACK):
+            leave_bank(t, slice(0, S))
+        h_small = [keep.tile([P, S], F32, name="h_small%d" % t) for t in range(PACK)]
+        for t in range(PACK):
+            nc.sync.dma_start(h_small[t][:], h_win[t][:, :S])
 
         ow = keep.tile([P, S], U32, name="ow", align_bytes=64)
         osc = keep.tile([P, S], U8, name="osc", align_bytes=64)
@@ -201,29 +238,31 @@ def tile_picked_joinminmxhingelap_none_po_kernel(
         def planes(c0, n, woven):
             cols = slice(c0, c0 + n)
             nc.vector.quantize_mx(ow[:, cols].bitcast(FP8X4), osc[:, cols], woven[:])
-            nc.sync.dma_start(words_of(out_1)[:, cols], ow[:, cols].bitcast(I32))
 
-        pending = None
-        for c0, n in CH2:
-            cols = slice(c0, c0 + n)
-            ks = slice(c0 // 16, (c0 + n) // 16)
-            tag = "_%d" % c0
-            g = f32_chunk("g" + tag, n)
-            o = f32_chunk("o" + tag, n)
-            woven = keep.tile([P, PACK * n], BF16, name="o_woven" + tag, align_bytes=64)
-            for t in range(PACK):
-                nc.vector.tensor_tensor(g[:, t, :], h_win[t][:].indirect(l5[:, ks]), h4[:, t, cols], ALU.subtract)
-            for t in range(PACK):
-                nc.vector.tensor_tensor(o[:, t, :], h_win[t][:].indirect(l6[:, ks]), g[:, t, :], ALU.add)
-            if pending is not None:
-                planes(*pending)
-            nc.sync.dma_start(out_rows[:, :, cols], o[:])
-            if c0 + n == S:
-                nc.vector.tensor_copy(weave(woven[:]), planar(o[:]))
-            else:
-                nc.scalar.copy(weave(woven[:]), planar(o[:]))
-            pending = (c0, n, woven)
-        planes(*pending)
+        g = f32_chunk("g", S)
+        for half in range(2):
+            cols = slice(HALF * half, HALF * half + HALF)
+            nc.vector.tensor_tensor(g[:, 0, cols], h_win[0][:].indirect(l5[:, 16 * half : 16 * half + 16]), h4[:, 0, cols], ALU.subtract)
+        for t in range(1, PACK):
+            nc.vector.tensor_tensor(g[:, t, :], h_win[t][:].indirect(l5[:]), h4[:, t, :], ALU.subtract)
+        o0 = f32_chunk("o0", HEAD)
+        for t in range(PACK):
+            nc.vector.tensor_tensor(o0[:, t, :], h_win[t][:].indirect(l6[:, : HEAD // 16]), g[:, t, :HEAD], ALU.add)
+            nc.sync.dma_start(out_rows[:, t, :HEAD], o0[:, t, :])
+        o_woven = [woven_tile("o_woven%d" % c0, n) for c0, n in PIECES]
+        for k in range(2):
+            c0, n = PIECES[k]
+            nc.scalar.copy(weave(o_woven[k][:]), planar(o0[:, :, c0 : c0 + n]))
+        o1 = f32_chunk("o1", S - HEAD)
+        for t in range(PACK):
+            nc.vector.tensor_tensor(o1[:, t, :], h_small[t][:].indirect(l6[:, HEAD // 16 :]), g[:, t, HEAD:], ALU.add)
+        nc.scalar.dma_start(out_rows[:, :, HEAD:], o1[:])
+        planes(*PIECES[0], o_woven[0])
+        nc.vector.tensor_copy(weave(o_woven[2][:]), planar(o1[:]))
+        planes(*PIECES[1], o_woven[1])
+        planes(*PIECES[2], o_woven[2])
+        nc.sync.dma_start(words_of(out_1)[:, :HALF], ow[:, :HALF].bitcast(I32))
+        nc.sync.dma_start(words_of(out_1)[:, HALF:], ow[:, HALF:].bitcast(I32))
         for q in range(4):
-            queue = nc.scalar if q % 2 else nc.sync
+            queue = nc.scalar if q % 2 == 0 else nc.sync
             queue.dma_start(out_2[0][4 * q : 4 * q + 4, :].bitcast(I32), osc[32 * q : 32 * q + 4, :].bitcast(I32))

@@ -64,6 +64,8 @@ def tile_picked_joinminmxhingelap_none_po_kernel(
         h_win = [keep.tile([P, 2 * S], F32, name="h_win%d" % t) for t in range(PACK)]
         for t in range(PACK):
             nc.vector.memset(y_win[t][:, S:], 0.0)
+        for t in range(PACK):
+            nc.vector.memset(h_win[t][:, S:], 0.0)
         xw = keep.tile([P, T], U32, name="xw", align_bytes=64)
         w1w_raw = keep.tile([P, S], I32, name="w1w_raw", align_bytes=64)
         w23w_raw = keep.tile([P, 2, S], I32, name="w23w_raw", align_bytes=64)
@@ -72,8 +74,8 @@ def tile_picked_joinminmxhingelap_none_po_kernel(
 
         offs_sb = load_list("offs_sb", offs)
         nc.sync.dma_start(w1w_raw[:], words_of(w1_words))
+        l1 = load_list("l1", n1)
         l3 = load_list("l3", n3)
-        l4 = load_list("l4", n4)
         nc.sync.dma_start(xw[:].bitcast(I32), words_of(x_words))
         load_scales(nc.sync, xs, x_scales, 0)
         load_scales(nc.gpsimd, w1s_raw, w1_scales, 0, (0, 1))
@@ -81,16 +83,14 @@ def tile_picked_joinminmxhingelap_none_po_kernel(
         nc.gpsimd.memset(w23s_raw[:].bitcast(I32), 0)
         ident = keep.tile([P, P], F32, name="ident")
         make_identity(nc, ident[:])
-        for t in range(PACK):
-            nc.gpsimd.memset(h_win[t][:, S:], 0.0)
-        l1 = load_list("l1", n1)
-        l2 = load_list("l2", n2)
-        nc.sync.dma_start(gm_sb[:], gm.rearrange("(p t) o -> p (t o)", t=PACK))
-        nc.sync.dma_start(gn_sb[:], gn.rearrange("(p t) o -> p (t o)", t=PACK))
+        l4 = load_list("l4", n4)
         nc.sync.dma_start(w23w_raw[:, 0, :], words_of(w2_words))
         nc.sync.dma_start(w23w_raw[:, 1, :], words_of(w3_words))
         load_scales(nc.sync, w23s_raw, w2_scales, 0)
         load_scales(nc.sync, w23s_raw, w3_scales, 4)
+        nc.sync.dma_start(gm_sb[:], gm.rearrange("(p t) o -> p (t o)", t=PACK))
+        l2 = load_list("l2", n2)
+        nc.sync.dma_start(gn_sb[:], gn.rearrange("(p t) o -> p (t o)", t=PACK))
         l5 = load_list("l5", n5)
         l6 = load_list("l6", n6)
 
@@ -132,10 +132,10 @@ def tile_picked_joinminmxhingelap_none_po_kernel(
 
         w23w = keep.tile([P, 2, S], I32, name="w23w", align_bytes=64)
         w23s = keep.tile([P, S], U8, name="w23s", align_bytes=64)
-        nc.gpsimd.tensor_copy(
+        nc.vector.tensor_copy(
             w23w[:].rearrange("p g (t m) -> p g m t", t=PACK), w23w_raw[:].rearrange("p g (m t) -> p g m t", t=PACK)
         )
-        nc.gpsimd.tensor_copy(w23s[:].rearrange("p (t m) -> p t m", t=PACK), w23s_raw[:].rearrange("p (m t) -> p t m", t=PACK))
+        nc.vector.tensor_copy(w23s[:].rearrange("p (t m) -> p t m", t=PACK), w23s_raw[:].rearrange("p (m t) -> p t m", t=PACK))
 
         h4 = keep.tile([P, PACK, S], F32, name="h4")
         zw = keep.tile([P, S], U32, name="zw", align_bytes=64)
@@ -149,6 +149,8 @@ def tile_picked_joinminmxhingelap_none_po_kernel(
         def woven_tile(name, n):
             return work.tile([P, PACK * n], BF16, name=name, tag=name, align_bytes=64)
 
+        a = f32_chunk("a", S)
+        nc.vector.tensor_copy(a[:, 0, :], y_win[0][:].indirect(l1[:]))
         c = f32_chunk("c", S)
         d = f32_chunk("d", S)
         z2_flat = work.tile([P, PACK, S], BF16, name="z2_flat", tag="z2_flat")
@@ -156,11 +158,10 @@ def tile_picked_joinminmxhingelap_none_po_kernel(
             hinges = []
             for got, lst, scale, name in ((c, l3, -1.0, "c"), (d, l4, 0.5, "d")):
                 diff = ring.tile([P, PACK, P], F32, name="diff", tag="ring")
-                nc.vector.tensor_copy(got[:, t, :], y_win[t][:].indirect(lst[:]))
+                nc.vector.tensor_tensor(got[:, t, :], y_win[t][:].indirect(lst[:]), neg_y[:, t, :], ALU.add)
                 for j in range(PACK):
                     js = slice(P * j, P * j + P)
-                    nc.tensor.matmul(diff[:, j, :], neg_y[:, t, js], ident[:], start=True, stop=False, is_transpose=True)
-                    nc.tensor.matmul(diff[:, j, :], got[:, t, js], ident[:], start=False, stop=True, is_transpose=True)
+                    nc.tensor.transpose(diff[:, j, :], got[:, t, js], ident[:])
                 hinge = work.tile([P, PACK, P], F32, name="hinge_%s%d" % (name, t))
                 nc.scalar.activation(hinge[:], diff[:], ACT.Relu, scale=scale)
                 hinges.append(hinge)
@@ -195,8 +196,7 @@ def tile_picked_joinminmxhingelap_none_po_kernel(
             nc.scalar.activation(h_win[t][:, cols], h_ps[t][:, cols], ACT.Copy, scale=0.75)
             nc.scalar.copy(h4[:, t, cols], h_ps[t][:, cols])
 
-        a = f32_chunk("a", S)
-        for t in range(PACK):
+        for t in range(1, PACK):
             nc.vector.tensor_copy(a[:, t, :], y_win[t][:].indirect(l1[:]))
         b0 = f32_chunk("b0", HEAD)
         z_flat = work.tile([P, PACK, HEAD], BF16, name="z_flat", tag="z2_flat")

@@ -58,14 +58,12 @@ def tile_picked_joinminmxhingelap_none_po_kernel(
         w1s_raw = keep.tile([P, S], U8, name="w1s_raw", align_bytes=64)
         w23s_raw = keep.tile([P, S], U8, name="w23s_raw", align_bytes=64)
         nc.gpsimd.memset(xs[:].bitcast(I32), 0)
-        nc.vector.memset(w1s_raw[:].bitcast(I32), 0)
+        nc.gpsimd.memset(w1s_raw[:].bitcast(I32), 0)
 
         y_win = [keep.tile([P, 2 * S], F32, name="y_win%d" % t) for t in range(PACK)]
         h_win = [keep.tile([P, 2 * S], F32, name="h_win%d" % t) for t in range(PACK)]
         for t in range(PACK):
             nc.vector.memset(y_win[t][:, S:], 0.0)
-        for t in range(PACK):
-            nc.vector.memset(h_win[t][:, S:], 0.0)
         xw = keep.tile([P, T], U32, name="xw", align_bytes=64)
         w1w_raw = keep.tile([P, S], I32, name="w1w_raw", align_bytes=64)
         w23w_raw = keep.tile([P, 2, S], I32, name="w23w_raw", align_bytes=64)
@@ -75,17 +73,16 @@ def tile_picked_joinminmxhingelap_none_po_kernel(
         offs_sb = load_list("offs_sb", offs)
         nc.sync.dma_start(w1w_raw[:], words_of(w1_words))
         l1 = load_list("l1", n1)
-        l3 = load_list("l3", n3)
-        nc.sync.dma_start(xw[:].bitcast(I32), words_of(x_words))
         load_scales(nc.sync, xs, x_scales, 0)
-        load_scales(nc.gpsimd, w1s_raw, w1_scales, 0, (0, 1))
-        load_scales(nc.sync, w1s_raw, w1_scales, 0, (2, 3))
+        nc.sync.dma_start(xw[:].bitcast(I32), words_of(x_words))
+        load_scales(nc.sync, w1s_raw, w1_scales, 0)
         nc.gpsimd.memset(w23s_raw[:].bitcast(I32), 0)
         ident = keep.tile([P, P], F32, name="ident")
         make_identity(nc, ident[:])
-        l4 = load_list("l4", n4)
+        l3 = load_list("l3", n3)
         nc.sync.dma_start(w23w_raw[:, 0, :], words_of(w2_words))
         nc.sync.dma_start(w23w_raw[:, 1, :], words_of(w3_words))
+        l4 = load_list("l4", n4)
         load_scales(nc.sync, w23s_raw, w2_scales, 0)
         load_scales(nc.sync, w23s_raw, w3_scales, 4)
         nc.sync.dma_start(gm_sb[:], gm.rearrange("(p t) o -> p (t o)", t=PACK))
@@ -93,6 +90,9 @@ def tile_picked_joinminmxhingelap_none_po_kernel(
         nc.sync.dma_start(gn_sb[:], gn.rearrange("(p t) o -> p (t o)", t=PACK))
         l5 = load_list("l5", n5)
         l6 = load_list("l6", n6)
+
+        for t in range(PACK):
+            nc.scalar.copy(h_win[t][:, S:], y_win[0][:, S:])
 
         w1w = keep.tile([P, S], I32, name="w1w", align_bytes=64)
         w1s = keep.tile([P, S], U8, name="w1s", align_bytes=64)

from contextlib import ExitStack

import concourse.mybir as mybir
from concourse.masks import make_identity

F32 = mybir.dt.float32
BF16 = mybir.dt.bfloat16
I32 = mybir.dt.int32
U32 = mybir.dt.uint32
U16 = mybir.dt.uint16
U8 = mybir.dt.uint8
FP8X4 = mybir.dt.float8_e4m3fn_x4
ALU = mybir.AluOpType
ACT = mybir.ActivationFunctionType

P = 128
PACK = 4
T = 2048
S = 512
FLOPS = 3 * 2 * 512 * 512 * 512
HALF = 256
HEAD = 384
PIECES = ((0, 256), (256, 128), (384, 128))


def words_of(ap):
    return ap[0].rearrange("p n t -> p (n t)").bitcast(I32)


def weave(flat):
    return flat.rearrange("p (c i t) -> p c t i", i=4, t=PACK)


def planar(tile3):
    return tile3.rearrange("p t (c i) -> p c t i", i=4)


def tile_picked_joinminmxhingelap_none_po_kernel(
    tc, x_words, x_scales, w1_words, w1_scales, gn, gm, w2_words, w2_scales, w3_words, w3_scales,
    offs, n1, n2, n3, n4, n5, n6, out_0, out_1, out_2,
):
    nc = tc.nc
    with ExitStack() as ctx:
        keep = ctx.enter_context(tc.tile_pool(name="keep", bufs=1))
        ring = ctx.enter_context(tc.psum_pool(name="ring", bufs=8))
        work = ctx.enter_context(tc.tile_pool(name="work", bufs=1))

        def load_list(name, src):
            tile = keep.tile([P, S // 16], U16, name=name)
            nc.sync.dma_start(tile[:], src)
            return tile

        def load_scales(queue, tile, src, k, quadrants=(0, 1, 2, 3)):
            for q in quadrants:
                queue.dma_start(tile[32 * q + k : 32 * q + k + 4, :].bitcast(I32), src[0][4 * q : 4 * q + 4, :].bitcast(I32))

        xs = keep.tile([P, T], U8, name="xs", align_bytes=64)
        w1s_raw = keep.tile([P, S], U8, name="w1s_raw", align_bytes=64)
        w23s_raw = keep.tile([P, S], U8, name="w23s_raw", align_bytes=64)
        nc.gpsimd.memset(xs[:].bitcast(I32), 0)
        nc.gpsimd.memset(w1s_raw[:].bitcast(I32), 0)

        y_win = [keep.tile([P, 2 * S], F32, name="y_win%d" % t) for t in range(PACK)]
        h_win = [keep.tile([P, 2 * S], F32, name="h_win%d" % t) for t in range(PACK)]
        for t in range(PACK):
            nc.vector.memset(y_win[t][:, S:], 0.0)
        xw = keep.tile([P, T], U32, name="xw", align_bytes=64)
        w1w_raw = keep.tile([P, S], I32, name="w1w_raw", align_bytes=64)
        w23w_raw = keep.tile([P, 2, S], I32, name="w23w_raw", align_bytes=64)
        gn_sb = keep.tile([P, PACK], F32, name="gn_sb")
        gm_sb = keep.tile([P, PACK], F32, name="gm_sb")

        offs_sb = load_list("offs_sb", offs)
        nc.sync.dma_start(w1w_raw[:], words_of(w1_words))
        l1 = load_list("l1", n1)
        load_scales(nc.sync, xs, x_scales, 0)
        nc.sync.dma_start(xw[:].bitcast(I32), words_of(x_words))
        load_scales(nc.sync, w1s_raw, w1_scales, 0)
        nc.gpsimd.memset(w23s_raw[:].bitcast(I32), 0)
        ident = keep.tile([P, P], F32, name="ident")
        make_identity(nc, ident[:])
        l3 = load_list("l3", n3)
        nc.sync.dma_start(w23w_raw[:, 0, :], words_of(w2_words))
        nc.sync.dma_start(w23w_raw[:, 1, :], words_of(w3_words))
        l4 = load_list("l4", n4)
        load_scales(nc.sync, w23s_raw, w2_scales, 0)
        load_scales(nc.sync, w23s_raw, w3_scales, 4)
        nc.sync.dma_start(gm_sb[:], gm.rearrange("(p t) o -> p (t o)", t=PACK))
        l2 = load_list("l2", n2)
        nc.sync.dma_start(gn_sb[:], gn.rearrange("(p t) o -> p (t o)", t=PACK))
        l5 = load_list("l5", n5)
        l6 = load_list("l6", n6)

        for t in range(PACK):
            nc.scalar.copy(h_win[t][:, S:], y_win[0][:, S:])

        w1w = keep.tile([P, S], I32, name="w1w", align_bytes=64)
        w1s = keep.tile([P, S], U8, name="w1s", align_bytes=64)
        nc.vector.tensor_copy(w1w[:].rearrange("p (t m) -> p m t", t=PACK), w1w_raw[:].rearrange("p (m t) -> p m t", t=PACK))
        nc.vector.tensor_copy(w1s[:].rearrange("p (t m) -> p t m", t=PACK), w1s_raw[:].rearrange("p (m t) -> p t m", t=PACK))

        xgs = keep.tile([P, S], U8, name="xgs", align_bytes=64)
        xgw = keep.tile([P, S], U32, name="xgw", align_bytes=64)
        nc.vector.tensor_copy(xgs[:], xs[:].indirect(offs_sb[:]))
        y_ps = [ring.tile([P, S], F32, name="y_ps%d" % t, tag="ring") for t in range(PACK)]
        neg_y = keep.tile([P, PACK, S], F32, name="neg_y")
        def first_product(t, cols):
            ms = slice(P * t, P * t + P)
            nc.tensor.matmul_mx(
                y_ps[t][:, cols], lhsT=w1w[:, ms].bitcast(FP8X4), lhsT_scale=w1s[:, ms],
                rhs=xgw[:, cols].bitcast(FP8X4), rhs_scale=xgs[:, cols], start=True, stop=True,
            )

        for half in range(2):
            cols = slice(256 * half, 256 * half + 256)
            nc.vector.tensor_copy(xgw[:, cols], xw[:].indirect(offs_sb[:, 16 * half : 16 * half + 16]))
            for t in range(2):
                first_product(t, cols)
        for t in range(2, PACK):
            first_product(t, slice(0, S))
        for half in range(2):
            cols = slice(256 * half, 256 * half + 256)
            nc.scalar.copy(y_win[0][:, cols], y_ps[0][:, cols])
        for t in range(PACK):
            if t > 0:
                nc.scalar.copy(y_win[t][:, :S], y_ps[t][:])
            nc.scalar.activation(neg_y[:, t, :], y_ps[t][:], ACT.Copy, scale=-1.0)

        y_small = [keep.tile([P, S], F32, name="y_small%d" % t) for t in range(PACK)]
        for t in range(PACK):
            nc.sync.dma_start(y_small[t][:], y_win[t][:, :S])

        w23w = keep.tile([P, 2, S], I32, name="w23w", align_bytes=64)
        w23s = keep.tile([P, S], U8, name="w23s", align_bytes=64)
        nc.vector.tensor_copy(
            w23w[:].rearrange("p g (t m) -> p g m t", t=PACK), w23w_raw[:].rearrange("p g (m t) -> p g m t", t=PACK)
        )
        nc.vector.tensor_copy(w23s[:].rearrange("p (t m) -> p t m", t=PACK), w23s_raw[:].rearrange("p (m t) -> p t m", t=PACK))

        h4 = keep.tile([P, PACK, S], F32, name="h4")
        zw = keep.tile([P, S], U32, name="zw", align_bytes=64)
        zs = keep.tile([P, S], U8, name="zs", align_bytes=64)
        z2w = keep.tile([P, S], U32, name="z2w", align_bytes=64)
        z2s = keep.tile([P, S], U8, name="z2s", align_bytes=64)

        def f32_chunk(name, n, tag=None):
            return work.tile([P, PACK, n], F32, name=name, tag=tag or name, align_bytes=64)

        def woven_tile(name, n):
            return work.tile([P, PACK * n], BF16, name=name, tag=name, align_bytes=64)

        a = f32_chunk("a", S)
        nc.vector.tensor_copy(a[:, 0, :], y_win[0][:].indirect(l1[:]))
        c = f32_chunk("c", S)
        d = f32_chunk("d", S)
        z2_flat = work.tile([P, PACK, S], BF16, name="z2_flat", tag="z2_flat")
        for t in range(PACK):
            hinges = []
            for got, lst, scale, name in ((c, l3, -1.0, "c"), (d, l4, 0.5, "d")):
                diff = ring.tile([P, PACK, P], F32, name="diff", tag="ring")
                nc.vector.tensor_tensor(got[:, t, :], y_win[t][:].indirect(lst[:]), neg_y[:, t, :], ALU.add)
                for j in range(PACK):
                    js = slice(P * j, P * j + P)
                    nc.tensor.transpose(diff[:, j, :], got[:, t, js], ident[:])
                hinge = work.tile([P, PACK, P], F32, name="hinge_%s%d" % (name, t))
                nc.scalar.activation(hinge[:], diff[:], ACT.Relu, scale=scale)
                hinges.append(hinge)
            back = ring.tile([P, S], F32, name="back", tag="ring")
            for j in range(PACK):
                for k in range(2):
                    nc.tensor.matmul(back[:, P * j : P * j + P], hinges[k][:, j, :], ident[:],
                                     start=k == 0, stop=k == 1, is_transpose=True)
            nc.scalar.activation(z2_flat[:, t, :], back[:], ACT.Copy, scale=gm_sb[:, t : t + 1])
        z2_woven = woven_tile("z2_woven", S)
        nc.scalar.copy(weave(z2_woven[:]), planar(z2_flat[:]))

        h_ps = [ring.tile([P, S], F32, name="h_ps%d" % t, tag="ring") for t in range(PACK)]

        def second_product(c0, n, z_woven):
            cols = slice(c0, c0 + n)
            nc.vector.quantize_mx(zw[:, cols].bitcast(FP8X4), zs[:, cols], z_woven[:])
            for t in range(PACK):
                ms = slice(P * t, P * t + P)
                nc.tensor.matmul_mx(
                    h_ps[t][:, cols], lhsT=w23w[:, 1, ms].bitcast(FP8X4), lhsT_scale=w23s[4:P, ms],
                    rhs=z2w[:, cols].bitcast(FP8X4), rhs_scale=z2s[:, cols], start=True, stop=False,
                )
            for t in range(PACK):
                ms = slice(P * t, P * t + P)
                nc.tensor.matmul_mx(
                    h_ps[t][:, cols], lhsT=w23w[:, 0, ms].bitcast(FP8X4), lhsT_scale=w23s[:, ms],
                    rhs=zw[:, cols].bitcast(FP8X4), rhs_scale=zs[:, cols], start=False, stop=True,
                )

        def leave_bank(t, cols):
            nc.scalar.activation(h_win[t][:, cols], h_ps[t][:, cols], ACT.Copy, scale=0.75)
            nc.scalar.copy(h4[:, t, cols], h_ps[t][:, cols])

        for t in range(1, PACK):
            nc.vector.tensor_copy(a[:, t, :], y_win[t][:].indirect(l1[:]))
        b0 = f32_chunk("b0", HEAD)
        z_flat = work.tile([P, PACK, HEAD], BF16, name="z_flat", tag="z2_flat")
        for t in range(PACK):
            nc.vector.tensor_copy(b0[:, t, :], y_win[t][:].indirect(l2[:, : HEAD // 16]))
            nc.vector.tensor_tensor(a[:, t, :], a[:, t, :], y_win[t][:, :S], ALU.max)
            if t > 0:
                nc.vector.tensor_tensor(b0[:, t - 1, :], b0[:, t - 1, :], a[:, t - 1, :HEAD], ALU.min)
        nc.vector.quantize_mx(z2w[:].bitcast(FP8X4), z2s[:], z2_woven[:])
        nc.vector.tensor_tensor(b0[:, 3, :], b0[:, 3, :], a[:, 3, :HEAD], ALU.min)
        for t in range(PACK):
            nc.scalar.activation(z_flat[:, t, :], b0[:, t, :], ACT.Copy, scale=gn_sb[:, t : t + 1])
        z_woven = [woven_tile("z_woven%d" % c0, n) for c0, n in PIECES]
        for k in range(2):
            c0, n = PIECES[k]
            nc.scalar.copy(weave(z_woven[k][:]), planar(z_flat[:, :, c0 : c0 + n]))
        b1 = f32_chunk("b1", S - HEAD, "z2_woven")
        for t in range(PACK):
            nc.vector.tensor_copy(b1[:, t, :], y_small[t][:].indirect(l2[:, HEAD // 16 :]))
        second_product(*PIECES[0], z_woven[0])
        low = f32_chunk("low", S - HEAD, "z_woven0")
        nc.vector.tensor_tensor(low[:], b1[:], a[:, :, HEAD:], ALU.min)
        second_product(*PIECES[1], z_woven[1])
        leave_bank(0, slice(0, HEAD))
        spread = gn_sb[:].rearrange("p (c t i) -> p c t i", c=1, i=1).to_broadcast([P, (S - HEAD) // 4, PACK, 4])
        nc.vector.tensor_tensor(weave(z_woven[2][:]), planar(low[:]), spread, ALU.mult)
        second_product(*PIECES[2], z_woven[2])
        leave_bank(0, slice(HEAD, S))
        for t in range(1, PACK):
            leave_bank(t, slice(0, S))
        h_small = [keep.tile([P, S], F32, name="h_small%d" % t) for t in range(PACK)]
        for t in range(PACK):
            nc.sync.dma_start(h_small[t][:], h_win[t][:, :S])

        ow = keep.tile([P, S], U32, name="ow", align_bytes=64)
        osc = keep.tile([P, S], U8, name="osc", align_bytes=64)
        out_rows = out_0.rearrange("(p t) j -> p t j", t=PACK)

        def planes(c0, n, woven):
            cols = slice(c0, c0 + n)
            nc.vector.quantize_mx(ow[:, cols].bitcast(FP8X4), osc[:, cols], woven[:])

        g = f32_chunk("g", S)
        for half in range(2):
            cols = slice(HALF * half, HALF * half + HALF)
            nc.vector.tensor_tensor(g[:, 0, cols], h_win[0][:].indirect(l5[:, 16 * half : 16 * half + 16]), h4[:, 0, cols], ALU.subtract)
        for t in range(1, PACK):
            nc.vector.tensor_tensor(g[:, t, :], h_win[t][:].indirect(l5[:]), h4[:, t, :], ALU.subtract)
        o0 = f32_chunk("o0", HEAD)
        for t in range(PACK):
            nc.vector.tensor_tensor(o0[:, t, :], h_win[t][:].indirect(l6[:, : HEAD // 16]), g[:, t, :HEAD], ALU.add)
            nc.sync.dma_start(out_rows[:, t, :HEAD], o0[:, t, :])
        o_woven = [woven_tile("o_woven%d" % c0, n) for c0, n in PIECES]
        for k in range(2):
            c0, n = PIECES[k]
            nc.scalar.copy(weave(o_woven[k][:]), planar(o0[:, :, c0 : c0 + n]))
        o1 = f32_chunk("o1", S - HEAD)
        for t in range(PACK):
            nc.vector.tensor_tensor(o1[:, t, :], h_small[t][:].indirect(l6[:, HEAD // 16 :]), g[:, t, HEAD:], ALU.add)
        nc.scalar.dma_start(out_rows[:, :, HEAD:], o1[:])
        planes(*PIECES[0], o_woven[0])
        nc.vector.tensor_copy(weave(o_woven[2][:]), planar(o1[:]))
        planes(*PIECES[1], o_woven[1])
        planes(*PIECES[2], o_woven[2])
        nc.sync.dma_start(words_of(out_1)[:, :HALF], ow[:, :HALF].bitcast(I32))
        nc.sync.dma_start(words_of(out_1)[:, HALF:], ow[:, HALF:].bitcast(I32))
        for q in range(4):
            queue = nc.scalar if q % 2 == 0 else nc.sync
            queue.dma_start(out_2[0][4 * q : 4 * q + 4, :].bitcast(I32), osc[32 * q : 32 * q + 4, :].bitcast(I32))
